import numpy as np
import ml_dtypes


def mxq(x, axis, fmt="e4m3"):
    dtype, down = {"e4m3": (ml_dtypes.float8_e4m3fn, 7), "e5m2": (ml_dtypes.float8_e5m2, 14)}[fmt]
    v = np.moveaxis(np.asarray(x, np.float32).astype(ml_dtypes.bfloat16).astype(np.float64), axis, -1)
    blocks = v.reshape(v.shape[:-1] + (-1, 32))
    amax = np.abs(blocks).max(-1, keepdims=True)
    byte = np.maximum(np.where(amax > 0, np.frexp(amax)[1] - 1 + 127, 0) - down, 1)
    scale = np.exp2(byte - 127.0)
    codes = (blocks / scale).astype(np.float32).astype(dtype).astype(np.float64)
    return np.moveaxis((codes * scale).reshape(v.shape), -1, axis)


WIDE = False


def mx_kscale(k):
    if not WIDE:
        return np.ones(k)
    levels = np.array([10, -10, 5, -5, 0])
    if k % 512:
        return np.exp2(np.random.permutation(np.resize(levels, k // 32))).repeat(32)
    a = np.empty((k // 512, 16))
    for p in range(k // 512):
        a[p, :8] = np.random.permutation(np.resize(levels, 8))
        for g in range(8):
            far = levels[np.abs(levels - a[p, g]) >= 10]
            a[p, g + 8] = far[np.random.randint(len(far))]
    return np.exp2(a.ravel()).repeat(32)


def f64(x):
    return np.asarray(x).astype(np.float64)


def striped(idx):
    return np.tile(idx.reshape(-1, 16).T, (8, 1)).astype(np.uint16)


def unstriped(offs):
    return offs[:16].T.reshape(-1).astype(np.int64)


def striped8(idx):
    return np.concatenate([x.reshape(-1, 16).T for x in idx]).astype(np.uint16)


def runs(offs, k):
    lists = np.stack([offs[16 * r : 16 * r + 16].T.reshape(-1) for r in range(8)]).astype(np.int64)
    return lists[np.arange(k) % 512 // 64]


def pack_weight(w):
    k, n = w.shape
    w = f64(np.asarray(w, np.float32).astype(ml_dtypes.bfloat16)).reshape(k // 32, 32, n)
    amax = np.abs(w).max(1)
    byte = np.clip(np.where(amax > 0, np.frexp(amax)[1] - 1 + 127 - 7, 1), 1, 254)
    scaled = (w * np.exp2(127.0 - byte)[:, None, :]).reshape(k, n).astype(np.float32)
    words = np.ascontiguousarray(scaled.reshape(k // 512, 128, 4, n).transpose(0, 1, 3, 2)).astype(ml_dtypes.float8_e4m3fn).view(np.uint8)
    return words, np.ascontiguousarray(byte.astype(np.uint8).reshape(k // 512, 16, n))


def unpack_weight(words, scales):
    g, p, n, _ = words.shape
    vals = np.ascontiguousarray(words).view(ml_dtypes.float8_e4m3fn).astype(np.float64) * np.repeat(np.exp2(scales.astype(np.float64) - 127.0), 8, axis=1)[..., None]
    return vals.transpose(0, 1, 3, 2).reshape(g * 512, n)


E2M1 = np.array([0.0, 0.5, 1.0, 1.5, 2.0, 3.0, 4.0, 6.0, -0.0, -0.5, -1.0, -1.5, -2.0, -3.0, -4.0, -6.0])


def pack_fp4(w):
    k, n = w.shape
    w = f64(np.asarray(w, np.float32).astype(ml_dtypes.bfloat16)).reshape(k // 32, 32, n)
    amax = np.abs(w).max(1)
    mant, ex = np.frexp(amax / 6.0)
    byte = np.clip(np.where(amax > 0, np.where(mant > 0.5, ex, ex - 1) + 127, 1), 1, 254)
    scaled = (w * np.exp2(127.0 - byte)[:, None, :]).reshape(k, n).astype(np.float32)
    c = np.ascontiguousarray(scaled.reshape(k // 512, 128, 4, n).transpose(0, 1, 3, 2)).astype(ml_dtypes.float4_e2m1fn).view(np.uint8) & 0xF
    words = (c[..., 0::2] | (c[..., 1::2] << 4)).reshape(k // 512, 128, 2 * n)
    return np.ascontiguousarray(words), np.ascontiguousarray(byte.astype(np.uint8).reshape(k // 512, 16, n))


def unpack_fp4(words, scales):
    g, _, n = scales.shape
    words = np.ascontiguousarray(words).reshape(g, 128, n, 2)
    nib = np.empty((g, 128, n, 4), np.uint8)
    nib[..., 0::2] = words & 0xF
    nib[..., 1::2] = words >> 4
    vals = E2M1[nib] * np.repeat(np.exp2(scales.astype(np.float64) - 127.0), 8, axis=1)[..., None]
    return vals.transpose(0, 1, 3, 2).reshape(g * 512, n)


def planes(y):
    n, m = y.shape
    v = y.astype(np.float32).astype(ml_dtypes.bfloat16).astype(np.float64).reshape(n // 32, 32, m)
    top = np.abs(v).max(1)
    byte = np.clip(np.where(top > 0, np.frexp(top)[1] - 1 + 127 - 7, 1), 1, 254)
    codes = (v * np.exp2(127.0 - byte)[:, None, :]).reshape(n, m).astype(np.float32).astype(ml_dtypes.float8_e4m3fn).view(np.uint8)
    words = codes.reshape(n // 512, 128, 4, m).transpose(0, 1, 3, 2)
    return np.ascontiguousarray(words), np.ascontiguousarray(byte.astype(np.uint8).reshape(n // 512, 16, m))


K, T, S, H, W, C = 512, 2048, 256, 512, 1024, 512


def setup_inputs():
    n = np.random.standard_normal
    s = mx_kscale(K)[:, None]
    packed_xT = pack_weight(n((K, T)) * s)
    packed_w1 = pack_fp4(n((K, H)) / np.sqrt(K) / s)
    return {
        "x_words": packed_xT[0],
        "x_scales": packed_xT[1],
        "w1_words": packed_w1[0],
        "w1_scales": packed_w1[1],
        "gs": (np.random.uniform(0.5, 1.5, (K, 1)) / s).astype(np.float32),
        "offs": striped8(np.random.randint(0, T, (8, S))),
        "n1": striped(np.random.randint(0, S, W)),
        "cand": striped8(np.random.randint(0, T, (8, C))),
        "n2": striped(np.random.permutation(S)),
        "n3": striped(np.random.permutation(S)),
        "n4": striped(np.random.permutation(S)),
    }


def reference(x_words, x_scales, w1_words, w1_scales, gs, offs, n1, cand, n2, n3, n4):
    x_cand = unpack_weight(x_words, x_scales)[np.arange(K)[:, None], runs(cand, K)]
    xq = unpack_weight(x_words, x_scales)[np.arange(K)[:, None], runs(offs, K)]
    y = unpack_fp4(w1_words, w1_scales).T @ xq
    mb = y[:, unstriped(n1)]
    mx = mb.reshape(H, S, 4).max(axis=2)
    mn = mb.reshape(H, S, 4).min(axis=2)
    z = f64(gs) * (np.maximum(np.minimum(1.5 * y, mx), mn))
    s = 0.0625 * ((x_cand.T @ mxq(z, 0, "e4m3")))
    out_0 = np.maximum(s, s[:, unstriped(n2)]) - (np.maximum(s[:, unstriped(n3)], s[:, unstriped(n4)]))
    return (out_0,) + planes(out_0)

@@ -1,0 +1,218 @@
+from contextlib import ExitStack
+
+import concourse.mybir as mybir
+
+K, T, S, H, W, C = 512, 2048, 256, 512, 1024, 512
+FLOPS = 2 * K * H * S + 2 * K * C * S
+
+F32 = mybir.dt.float32
+BF16 = mybir.dt.bfloat16
+I32 = mybir.dt.int32
+U32 = mybir.dt.uint32
+U16 = mybir.dt.uint16
+U8 = mybir.dt.uint8
+FP8X4 = mybir.dt.float8_e4m3fn_x4
+FP4X4 = mybir.dt.float4_e2m1fn_x4
+ALU = mybir.AluOpType
+COPY = mybir.ActivationFunctionType.Copy
+
+P = 128
+PACK = 4
+HALF = S // 2
+MEMBERS = W // S
+Z_PIECES = ((0, 64), (64, 128), (192, 64))
+OUT_PIECES = ((0, 128), (128, 64), (192, 64))
+Y_WINDOW = MEMBERS * HALF + 16
+
+
+def tile_picked_hcandgclipmix_none_po_kernel(
+    tc, x_words, x_scales, w1_words, w1_scales, gs, offs, n1, cand, n2, n3, n4, out_0, out_1, out_2
+):
+    nc = tc.nc
+    with ExitStack() as ctx:
+        keep = ctx.enter_context(tc.tile_pool(name="keep", bufs=1))
+        psum = ctx.enter_context(tc.psum_pool(name="psum", bufs=1))
+
+        def tile(name, shape, dtype):
+            return keep.tile(shape, dtype, name=name, align_bytes=64)
+
+        def load_list(name, src):
+            t = keep.tile(list(src.shape), U16, name=name)
+            nc.sync.dma_start(t[:], src)
+            return t
+
+        def place_scale_rows(plane, spread):
+            for i in range(4):
+                nc.sync.dma_start(plane[i:P:32, :].bitcast(I32), spread[8 * i : P : 32, :].bitcast(I32))
+
+        x_bytes = tile("x_bytes", [P, T], U8)
+        nc.gpsimd.memset(x_bytes[:].bitcast(I32), 0)
+        w_bytes = tile("w_bytes", [P, H], U8)
+        nc.vector.memset(w_bytes[:].bitcast(I32), 0)
+        xq_plane = tile("xq_plane", [P, S], U8)
+        nc.vector.memset(xq_plane[:].bitcast(I32), 0)
+        xc_plane = tile("xc_plane", [P, C], U8)
+        nc.vector.memset(xc_plane[:].bitcast(I32), 0)
+
+        x_codes = tile("x_codes", [P, T], I32)
+        nc.scalar.dma_start(x_codes[:], x_words[0].rearrange("p n r -> p (n r)").bitcast(I32))
+        offs_t = load_list("offs_t", offs)
+        nc.sync.dma_start(x_bytes[0:P:8, :].bitcast(I32), x_scales[0].bitcast(I32))
+        w_codes = tile("w_codes", [P, 2 * H], U8)
+        nc.sync.dma_start(w_codes[:].bitcast(I32), w1_words[0].bitcast(I32))
+        for q in range(4):
+            nc.scalar.dma_start(
+                w_bytes[32 * q : 32 * q + 4, :].bitcast(I32), w1_scales[0, 4 * q : 4 * q + 4, :].bitcast(I32)
+            )
+        cand_t = load_list("cand_t", cand)
+        gs_t = tile("gs_t", [P, PACK], F32)
+        n1_t = load_list("n1_t", n1)
+
+        y = [tile("y%d" % t, [P, Y_WINDOW], F32) for t in range(PACK)]
+        for t in range(PACK):
+            nc.gpsimd.memset(y[t][:, S:Y_WINDOW], 0.0)
+        nc.gpsimd.dma_start(gs_t[:], gs.rearrange("(p t) o -> p (t o)", t=PACK))
+
+        xq_bytes = tile("xq_bytes", [P, S], U8)
+        nc.vector.tensor_copy(xq_bytes[:], x_bytes[:].indirect(offs_t[:]))
+        place_scale_rows(xq_plane, xq_bytes)
+
+        w_dealt = tile("w_dealt", [P, 2 * H], U8)
+        nc.vector.tensor_copy(
+            w_dealt[:].rearrange("p (t m b) -> p m t b", t=PACK, b=2),
+            w_codes[:].rearrange("p (m t b) -> p m t b", t=PACK, b=2),
+        )
+        w_plane = tile("w_plane", [P, H], U8)
+        nc.vector.tensor_copy(
+            w_plane[:].rearrange("p (t m) -> p m t", t=PACK), w_bytes[:].rearrange("p (m t) -> p m t", t=PACK)
+        )
+
+        xq_codes = tile("xq_codes", [P, S], U32)
+        nc.vector.tensor_copy(xq_codes[:], x_codes[:].bitcast(U32).indirect(offs_t[:]))
+
+        xc_bytes = tile("xc_bytes", [P, C], U8)
+        nc.vector.tensor_copy(xc_bytes[:], x_bytes[:].indirect(cand_t[:]))
+        xc_bytes_dealt = tile("xc_bytes_dealt", [P, C], U8)
+        nc.vector.tensor_copy(
+            xc_bytes_dealt[:].rearrange("p (t m) -> p m t", t=PACK),
+            xc_bytes[:].rearrange("p (m t) -> p m t", t=PACK),
+        )
+        place_scale_rows(xc_plane, xc_bytes_dealt)
+
+        y_banks = []
+        for t in range(PACK):
+            y_bank = psum.tile([P, S], F32, name="y_bank%d" % t)
+            nc.tensor.matmul_mx(
+                out=y_bank[:],
+                lhsT=w_dealt[:, 2 * P * t : 2 * P * (t + 1)].bitcast(FP4X4),
+                lhsT_scale=w_plane[:, P * t : P * (t + 1)],
+                rhs=xq_codes[:].bitcast(FP8X4),
+                rhs_scale=xq_plane[:],
+                start=True,
+                stop=True,
+            )
+            y_banks.append(y_bank)
+
+        xc_codes = tile("xc_codes", [P, C], U32)
+        nc.vector.tensor_copy(xc_codes[:], x_codes[:].bitcast(U32).indirect(cand_t[:]))
+        xc_dealt = tile("xc_dealt", [P, C], U32)
+        nc.vector.tensor_copy(
+            xc_dealt[:].rearrange("p (t m) -> p m t", t=PACK), xc_codes[:].rearrange("p (m t) -> p m t", t=PACK)
+        )
+
+        n2_t = load_list("n2_t", n2)
+        n3_t = load_list("n3_t", n3)
+        n4_t = load_list("n4_t", n4)
+
+        z_codes = tile("z_codes", [P, S], U32)
+        z_plane = tile("z_plane", [P, S], U8)
+        for h, (j0, n) in enumerate(Z_PIECES):
+            cols = slice(j0, j0 + n)
+            list_cols = slice(MEMBERS * j0 // 16, MEMBERS * (j0 + n) // 16)
+            capped = tile("capped%d" % h, [P, PACK, n], F32)
+            least = tile("least%d" % h, [P, PACK, n], F32)
+            for t in range(PACK):
+                if h == 0:
+                    nc.scalar.activation(y[t][:, 0:S], y_banks[t][:], COPY, scale=gs_t[:, t : t + 1])
+                members = tile("members%d%d" % (h, t), [P, n, 2, 2], F32)
+                nc.scalar.activation(
+                    members[:].rearrange("p j a b -> p (j a b)"), y[t][:].indirect(n1_t[:, list_cols]), COPY
+                )
+                pair_max = tile("pair_max%d%d" % (h, t), [P, n, 2], F32)
+                pair_min = tile("pair_min%d%d" % (h, t), [P, n, 2], F32)
+                nc.vector.tensor_tensor(pair_max[:], members[:, :, 0, :], members[:, :, 1, :], ALU.max)
+                nc.vector.tensor_tensor(pair_min[:], members[:, :, 0, :], members[:, :, 1, :], ALU.min)
+                most = tile("most%d%d" % (h, t), [P, n], F32)
+                nc.vector.tensor_tensor(most[:], pair_max[:, :, 0], pair_max[:, :, 1], ALU.max)
+                nc.vector.tensor_tensor(least[:, t, :], pair_min[:, :, 0], pair_min[:, :, 1], ALU.min)
+                nc.vector.scalar_tensor_tensor(capped[:, t, :], y[t][:, cols], 1.5, most[:], ALU.mult, ALU.min)
+            z = tile("z%d" % h, [P, n, PACK], BF16)
+            nc.vector.tensor_tensor(
+                z[:].rearrange("p (c i) t -> p c t i", i=4),
+                capped[:].rearrange("p t (c i) -> p c t i", i=4),
+                least[:].rearrange("p t (c i) -> p c t i", i=4),
+                ALU.max,
+            )
+            nc.vector.quantize_mx(
+                out=z_codes[:, cols].bitcast(FP8X4), scales=z_plane[:, cols], in_=z[:].rearrange("p j t -> p (j t)")
+            )
+
+        s = tile("s", [P, PACK, S], F32)
+        for h in range(2):
+            cols = slice(h * HALF, (h + 1) * HALF)
+            for pair in range(2):
+                s_bank = psum.tile([P, 2, HALF], F32, name="s_bank%d%d" % (h, pair))
+                for u in range(2):
+                    t = 2 * pair + u
+                    nc.tensor.matmul_mx(
+                        out=s_bank[:, u, :],
+                        lhsT=xc_dealt[:, P * t : P * (t + 1)].bitcast(FP8X4),
+                        lhsT_scale=xc_plane[:, P * t : P * (t + 1)],
+                        rhs=z_codes[:, cols].bitcast(FP8X4),
+                        rhs_scale=z_plane[:, cols],
+                        start=True,
+                        stop=True,
+                    )
+                if h == 1 and pair == 1:
+                    nc.vector.tensor_scalar(s[:, 2:4, cols], s_bank[:], 0.0625, None, ALU.mult)
+                else:
+                    nc.scalar.activation(s[:, 2 * pair : 2 * pair + 2, cols], s_bank[:], COPY, scale=0.0625)
+
+        out_rows = out_0.rearrange("(p t) j -> p t j", t=PACK)
+        out_words = out_1[0].rearrange("p j r -> p (j r)").bitcast(I32)
+        out_plane = tile("out_plane", [P, S], U8)
+        for h, (j0, n) in enumerate(OUT_PIECES):
+            cols = slice(j0, j0 + n)
+            list_cols = slice(j0 // 16, (j0 + n) // 16)
+            s2 = tile("s2_%d" % h, [P, PACK, n], F32)
+            s3 = tile("s3_%d" % h, [P, PACK, n], F32)
+            s4 = tile("s4_%d" % h, [P, PACK, n], F32)
+            for t in range(PACK):
+                nc.vector.tensor_copy(s2[:, t, :], s[:, t, :].indirect(n2_t[:, list_cols]))
+            for t in range(PACK):
+                nc.scalar.activation(s3[:, t, :], s[:, t, :].indirect(n3_t[:, list_cols]), COPY)
+                nc.scalar.activation(s4[:, t, :], s[:, t, :].indirect(n4_t[:, list_cols]), COPY)
+            first = tile("first%d" % h, [P, PACK, n], F32)
+            nc.vector.tensor_tensor(first[:], s[:, :, cols], s2[:], ALU.max)
+            second = tile("second%d" % h, [P, PACK, n], F32)
+            nc.vector.tensor_tensor(second[:], s3[:], s4[:], ALU.max)
+            result = tile("result%d" % h, [P, PACK, n], F32)
+            nc.vector.tensor_tensor(result[:], first[:], second[:], ALU.subtract)
+            nc.sync.dma_start(out_rows[:, :, cols], result[:])
+            rounded = tile("rounded%d" % h, [P, n, PACK], BF16)
+            nc.vector.tensor_copy(
+                rounded[:].rearrange("p (c i) t -> p c t i", i=4),
+                result[:].rearrange("p t (c i) -> p c t i", i=4),
+            )
+            out_codes = tile("out_codes%d" % h, [P, n], U32)
+            nc.vector.quantize_mx(
+                out=out_codes[:].bitcast(FP8X4),
+                scales=out_plane[:, cols],
+                in_=rounded[:].rearrange("p j t -> p (j t)"),
+            )
+            nc.sync.dma_start(out_words[:, cols], out_codes[:].bitcast(I32))
+        for q in range(4):
+            queue = nc.scalar if q % 2 else nc.sync
+            queue.dma_start(
+                out_2[0, 4 * q : 4 * q + 4, :].bitcast(I32), out_plane[32 * q : 32 * q + 4, :].bitcast(I32)
+            )

@@ -20,7 +20,7 @@ P = 128
 PACK = 4
 HALF = S // 2
 MEMBERS = W // S
-Z_PIECES = ((0, 64), (64, 128), (192, 64))
+QUARTER = S // 4
 OUT_PIECES = ((0, 128), (128, 64), (192, 64))
 Y_WINDOW = MEMBERS * HALF + 16
 
@@ -41,41 +41,42 @@ def tile_picked_hcandgclipmix_none_po_kernel(
             nc.sync.dma_start(t[:], src)
             return t
 
-        def place_scale_rows(plane, spread):
+        def place_scale_rows(queues, plane, spread):
             for i in range(4):
-                nc.sync.dma_start(plane[i:P:32, :].bitcast(I32), spread[8 * i : P : 32, :].bitcast(I32))
+                queues[i % len(queues)].dma_start(plane[i:P:32, :].bitcast(I32), spread[8 * i : P : 32, :].bitcast(I32))
 
+        w_bytes = tile("w_bytes", [P, H], U8)
+        nc.gpsimd.memset(w_bytes[:].bitcast(I32), 0)
         x_bytes = tile("x_bytes", [P, T], U8)
         nc.gpsimd.memset(x_bytes[:].bitcast(I32), 0)
-        w_bytes = tile("w_bytes", [P, H], U8)
-        nc.vector.memset(w_bytes[:].bitcast(I32), 0)
         xq_plane = tile("xq_plane", [P, S], U8)
         nc.vector.memset(xq_plane[:].bitcast(I32), 0)
         xc_plane = tile("xc_plane", [P, C], U8)
         nc.vector.memset(xc_plane[:].bitcast(I32), 0)
+        y = [tile("y%d" % t, [P, Y_WINDOW], F32) for t in range(PACK)]
+        for t in range(PACK):
+            nc.vector.memset(y[t][:, S:Y_WINDOW], 0.0)
+        s = tile("s", [P, (PACK + 1) * S], F32)
+        nc.vector.memset(s[:, PACK * S :], 0.0)
 
-        x_codes = tile("x_codes", [P, T], I32)
-        nc.scalar.dma_start(x_codes[:], x_words[0].rearrange("p n r -> p (n r)").bitcast(I32))
         offs_t = load_list("offs_t", offs)
         nc.sync.dma_start(x_bytes[0:P:8, :].bitcast(I32), x_scales[0].bitcast(I32))
         w_codes = tile("w_codes", [P, 2 * H], U8)
         nc.sync.dma_start(w_codes[:].bitcast(I32), w1_words[0].bitcast(I32))
+        x_codes = tile("x_codes", [P, T], I32)
+        nc.sync.dma_start(x_codes[:], x_words[0].rearrange("p n r -> p (n r)").bitcast(I32))
+        cand_t = load_list("cand_t", cand)
+        n1_t = load_list("n1_t", n1)
         for q in range(4):
             nc.scalar.dma_start(
                 w_bytes[32 * q : 32 * q + 4, :].bitcast(I32), w1_scales[0, 4 * q : 4 * q + 4, :].bitcast(I32)
             )
-        cand_t = load_list("cand_t", cand)
         gs_t = tile("gs_t", [P, PACK], F32)
-        n1_t = load_list("n1_t", n1)
-
-        y = [tile("y%d" % t, [P, Y_WINDOW], F32) for t in range(PACK)]
-        for t in range(PACK):
-            nc.gpsimd.memset(y[t][:, S:Y_WINDOW], 0.0)
         nc.gpsimd.dma_start(gs_t[:], gs.rearrange("(p t) o -> p (t o)", t=PACK))
 
         xq_bytes = tile("xq_bytes", [P, S], U8)
         nc.vector.tensor_copy(xq_bytes[:], x_bytes[:].indirect(offs_t[:]))
-        place_scale_rows(xq_plane, xq_bytes)
+        place_scale_rows((nc.scalar, nc.sync), xq_plane, xq_bytes)
 
         w_dealt = tile("w_dealt", [P, 2 * H], U8)
         nc.vector.tensor_copy(
@@ -83,8 +84,8 @@ def tile_picked_hcandgclipmix_none_po_kernel(
             w_codes[:].rearrange("p (m t b) -> p m t b", t=PACK, b=2),
         )
         w_plane = tile("w_plane", [P, H], U8)
-        nc.vector.tensor_copy(
-            w_plane[:].rearrange("p (t m) -> p m t", t=PACK), w_bytes[:].rearrange("p (m t) -> p m t", t=PACK)
+        nc.gpsimd.tensor_copy(
+            w_plane[:].rearrange("p (t m) -> p t m", t=PACK), w_bytes[:].rearrange("p (m t) -> p t m", t=PACK)
         )
 
         xq_codes = tile("xq_codes", [P, S], U32)
@@ -97,7 +98,7 @@ def tile_picked_hcandgclipmix_none_po_kernel(
             xc_bytes_dealt[:].rearrange("p (t m) -> p m t", t=PACK),
             xc_bytes[:].rearrange("p (m t) -> p m t", t=PACK),
         )
-        place_scale_rows(xc_plane, xc_bytes_dealt)
+        place_scale_rows((nc.sync,), xc_plane, xc_bytes_dealt)
 
         y_banks = []
         for t in range(PACK):
@@ -126,38 +127,70 @@ def tile_picked_hcandgclipmix_none_po_kernel(
 
         z_codes = tile("z_codes", [P, S], U32)
         z_plane = tile("z_plane", [P, S], U8)
-        for h, (j0, n) in enumerate(Z_PIECES):
-            cols = slice(j0, j0 + n)
+        capped = tile("capped", [P, PACK, S], F32)
+        least = tile("least", [P, PACK, S], F32)
+        most = tile("most", [P, PACK, S], F32)
+        z = tile("z", [P, S, PACK], BF16)
+
+        def pair_up(t, j0, n):
+            name = "%d_%d" % (t, j0)
+            members = tile("members" + name, [P, n, 2, 2], F32)
             list_cols = slice(MEMBERS * j0 // 16, MEMBERS * (j0 + n) // 16)
-            capped = tile("capped%d" % h, [P, PACK, n], F32)
-            least = tile("least%d" % h, [P, PACK, n], F32)
-            for t in range(PACK):
-                if h == 0:
-                    nc.scalar.activation(y[t][:, 0:S], y_banks[t][:], COPY, scale=gs_t[:, t : t + 1])
-                members = tile("members%d%d" % (h, t), [P, n, 2, 2], F32)
-                nc.scalar.activation(
-                    members[:].rearrange("p j a b -> p (j a b)"), y[t][:].indirect(n1_t[:, list_cols]), COPY
-                )
-                pair_max = tile("pair_max%d%d" % (h, t), [P, n, 2], F32)
-                pair_min = tile("pair_min%d%d" % (h, t), [P, n, 2], F32)
-                nc.vector.tensor_tensor(pair_max[:], members[:, :, 0, :], members[:, :, 1, :], ALU.max)
-                nc.vector.tensor_tensor(pair_min[:], members[:, :, 0, :], members[:, :, 1, :], ALU.min)
-                most = tile("most%d%d" % (h, t), [P, n], F32)
-                nc.vector.tensor_tensor(most[:], pair_max[:, :, 0], pair_max[:, :, 1], ALU.max)
-                nc.vector.tensor_tensor(least[:, t, :], pair_min[:, :, 0], pair_min[:, :, 1], ALU.min)
-                nc.vector.scalar_tensor_tensor(capped[:, t, :], y[t][:, cols], 1.5, most[:], ALU.mult, ALU.min)
-            z = tile("z%d" % h, [P, n, PACK], BF16)
+            nc.scalar.activation(
+                members[:].rearrange("p j a b -> p (j a b)"), y[t][:].indirect(n1_t[:, list_cols]), COPY
+            )
+            pair_max = tile("pair_max" + name, [P, n, 2], F32)
+            pair_min = tile("pair_min" + name, [P, n, 2], F32)
+            nc.vector.tensor_tensor(pair_max[:], members[:, :, 0, :], members[:, :, 1, :], ALU.max)
+            nc.vector.tensor_tensor(pair_min[:], members[:, :, 0, :], members[:, :, 1, :], ALU.min)
+            return pair_max, pair_min
+
+        def extremes(t, j0, n, pair_max, pair_min):
+            cols = slice(j0, j0 + n)
+            nc.vector.tensor_tensor(most[:, t, cols], pair_max[:, :, 0], pair_max[:, :, 1], ALU.max)
+            nc.vector.tensor_tensor(least[:, t, cols], pair_min[:, :, 0], pair_min[:, :, 1], ALU.min)
+
+        def cap(t, j0, n):
+            cols = slice(j0, j0 + n)
+            nc.vector.scalar_tensor_tensor(capped[:, t, cols], y[t][:, cols], 1.5, most[:, t, cols], ALU.mult, ALU.min)
+
+        def floor_and_round(j0, n):
+            cols = slice(j0, j0 + n)
             nc.vector.tensor_tensor(
-                z[:].rearrange("p (c i) t -> p c t i", i=4),
-                capped[:].rearrange("p t (c i) -> p c t i", i=4),
-                least[:].rearrange("p t (c i) -> p c t i", i=4),
+                z[:, cols, :].rearrange("p (c i) t -> p c t i", i=4),
+                capped[:, :, cols].rearrange("p t (c i) -> p c t i", i=4),
+                least[:, :, cols].rearrange("p t (c i) -> p c t i", i=4),
                 ALU.max,
             )
+
+        def quantise(j0, n):
+            cols = slice(j0, j0 + n)
             nc.vector.quantize_mx(
-                out=z_codes[:, cols].bitcast(FP8X4), scales=z_plane[:, cols], in_=z[:].rearrange("p j t -> p (j t)")
+                out=z_codes[:, cols].bitcast(FP8X4),
+                scales=z_plane[:, cols],
+                in_=z[:, cols, :].rearrange("p j t -> p (j t)"),
             )
 
-        s = tile("s", [P, PACK, S], F32)
+        steps = [(t, 0, HALF) for t in range(PACK)] + [(t, HALF, HALF) for t in range(PACK - 1)]
+        steps = steps + [(PACK - 1, HALF, QUARTER), (PACK - 1, HALF + QUARTER, QUARTER)]
+        for i, (t, j0, n) in enumerate(steps):
+            if j0 == 0:
+                nc.scalar.activation(y[t][:, 0:S], y_banks[t][:], COPY, scale=gs_t[:, t : t + 1])
+            pairs = pair_up(t, j0, n)
+            if i > 0:
+                cap(*steps[i - 1])
+            extremes(t, j0, n, *pairs)
+            if i == PACK:
+                floor_and_round(0, HALF)
+            if i == PACK + 1:
+                quantise(0, HALF)
+        floor_and_round(HALF, QUARTER)
+        cap(*steps[-1])
+        quantise(HALF, QUARTER)
+        floor_and_round(HALF + QUARTER, QUARTER)
+        quantise(HALF + QUARTER, QUARTER)
+
+        s_rows = s[:, 0 : PACK * S].rearrange("p (t j) -> p t j", t=PACK)
         for h in range(2):
             cols = slice(h * HALF, (h + 1) * HALF)
             for pair in range(2):
@@ -174,45 +207,52 @@ def tile_picked_hcandgclipmix_none_po_kernel(
                         stop=True,
                     )
                 if h == 1 and pair == 1:
-                    nc.vector.tensor_scalar(s[:, 2:4, cols], s_bank[:], 0.0625, None, ALU.mult)
+                    nc.vector.tensor_scalar(s_rows[:, 2:4, cols], s_bank[:], 0.0625, None, ALU.mult)
                 else:
-                    nc.scalar.activation(s[:, 2 * pair : 2 * pair + 2, cols], s_bank[:], COPY, scale=0.0625)
+                    nc.scalar.activation(s_rows[:, 2 * pair : 2 * pair + 2, cols], s_bank[:], COPY, scale=0.0625)
 
         out_rows = out_0.rearrange("(p t) j -> p t j", t=PACK)
         out_words = out_1[0].rearrange("p j r -> p (j r)").bitcast(I32)
+        out_codes = tile("out_codes", [P, S], U32)
         out_plane = tile("out_plane", [P, S], U8)
+        s2 = tile("s2", [P, PACK, S], F32)
+        s3 = tile("s3", [P, PACK, S], F32)
+        for t in range(PACK):
+            window = s[:, t * S : (t + 2) * S]
+            nc.vector.tensor_copy(s2[:, t, :], window.indirect(n2_t[:]))
+            nc.scalar.activation(s3[:, t, :], window.indirect(n3_t[:]), COPY)
+        first = tile("first", [P, PACK, S], F32)
+        nc.vector.tensor_tensor(first[:], s_rows, s2[:], ALU.max)
+        results = []
         for h, (j0, n) in enumerate(OUT_PIECES):
             cols = slice(j0, j0 + n)
             list_cols = slice(j0 // 16, (j0 + n) // 16)
-            s2 = tile("s2_%d" % h, [P, PACK, n], F32)
-            s3 = tile("s3_%d" % h, [P, PACK, n], F32)
             s4 = tile("s4_%d" % h, [P, PACK, n], F32)
             for t in range(PACK):
-                nc.vector.tensor_copy(s2[:, t, :], s[:, t, :].indirect(n2_t[:, list_cols]))
-            for t in range(PACK):
-                nc.scalar.activation(s3[:, t, :], s[:, t, :].indirect(n3_t[:, list_cols]), COPY)
-                nc.scalar.activation(s4[:, t, :], s[:, t, :].indirect(n4_t[:, list_cols]), COPY)
-            first = tile("first%d" % h, [P, PACK, n], F32)
-            nc.vector.tensor_tensor(first[:], s[:, :, cols], s2[:], ALU.max)
+                nc.scalar.activation(s4[:, t, :], s_rows[:, t, :].indirect(n4_t[:, list_cols]), COPY)
             second = tile("second%d" % h, [P, PACK, n], F32)
-            nc.vector.tensor_tensor(second[:], s3[:], s4[:], ALU.max)
+            nc.vector.tensor_tensor(second[:], s3[:, :, cols], s4[:], ALU.max)
             result = tile("result%d" % h, [P, PACK, n], F32)
-            nc.vector.tensor_tensor(result[:], first[:], second[:], ALU.subtract)
+            nc.vector.tensor_tensor(result[:], first[:, :, cols], second[:], ALU.subtract)
             nc.sync.dma_start(out_rows[:, :, cols], result[:])
+            results.append(result)
+        for h, (j0, n) in enumerate(OUT_PIECES):
+            cols = slice(j0, j0 + n)
             rounded = tile("rounded%d" % h, [P, n, PACK], BF16)
-            nc.vector.tensor_copy(
-                rounded[:].rearrange("p (c i) t -> p c t i", i=4),
-                result[:].rearrange("p t (c i) -> p c t i", i=4),
-            )
-            out_codes = tile("out_codes%d" % h, [P, n], U32)
+            woven = rounded[:].rearrange("p (c i) t -> p c t i", i=4)
+            planar = results[h][:].rearrange("p t (c i) -> p c t i", i=4)
+            if h < len(OUT_PIECES) - 1:
+                nc.scalar.copy(woven, planar)
+            else:
+                nc.vector.tensor_copy(woven, planar)
             nc.vector.quantize_mx(
-                out=out_codes[:].bitcast(FP8X4),
+                out=out_codes[:, cols].bitcast(FP8X4),
                 scales=out_plane[:, cols],
                 in_=rounded[:].rearrange("p j t -> p (j t)"),
             )
-            nc.sync.dma_start(out_words[:, cols], out_codes[:].bitcast(I32))
+        nc.sync.dma_start(out_words, out_codes[:].bitcast(I32))
         for q in range(4):
-            queue = nc.scalar if q % 2 else nc.sync
+            queue = nc.sync if q == 3 else nc.scalar
             queue.dma_start(
                 out_2[0, 4 * q : 4 * q + 4, :].bitcast(I32), out_plane[32 * q : 32 * q + 4, :].bitcast(I32)
             )

@@ -18,11 +18,12 @@ COPY = mybir.ActivationFunctionType.Copy
 
 P = 128
 PACK = 4
-HALF = S // 2
 MEMBERS = W // S
+HALF = S // 2
 QUARTER = S // 4
-OUT_PIECES = ((0, 128), (128, 64), (192, 64))
 Y_WINDOW = MEMBERS * HALF + 16
+Y_TILES_ON_VECTOR = (1, 2)
+OUT_PIECES = ((0, 128), (128, 64), (192, 64))
 
 
 def tile_picked_hcandgclipmix_none_po_kernel(
@@ -37,24 +38,21 @@ def tile_picked_hcandgclipmix_none_po_kernel(
             return keep.tile(shape, dtype, name=name, align_bytes=64)
 
         def load_list(name, src):
-            t = keep.tile(list(src.shape), U16, name=name)
-            nc.sync.dma_start(t[:], src)
-            return t
+            offsets = keep.tile(list(src.shape), U16, name=name)
+            nc.sync.dma_start(offsets[:], src)
+            return offsets
 
-        def place_scale_rows(queues, plane, spread):
-            for i in range(4):
-                queues[i % len(queues)].dma_start(plane[i:P:32, :].bitcast(I32), spread[8 * i : P : 32, :].bitcast(I32))
+        def close_up_rows(plane, spread):
+            for i, queue in ((1, nc.sync), (2, nc.scalar), (3, nc.sync)):
+                queue.dma_start(plane[i:P:32, :].bitcast(I32), spread[8 * i : P : 32, :].bitcast(I32))
 
         w_bytes = tile("w_bytes", [P, H], U8)
         nc.gpsimd.memset(w_bytes[:].bitcast(I32), 0)
         x_bytes = tile("x_bytes", [P, T], U8)
-        nc.gpsimd.memset(x_bytes[:].bitcast(I32), 0)
-        xq_plane = tile("xq_plane", [P, S], U8)
-        nc.vector.memset(xq_plane[:].bitcast(I32), 0)
-        xc_plane = tile("xc_plane", [P, C], U8)
-        nc.vector.memset(xc_plane[:].bitcast(I32), 0)
+        nc.vector.memset(x_bytes[:, : 3 * T // 4].bitcast(I32), 0)
+        nc.gpsimd.memset(x_bytes[:, 3 * T // 4 :].bitcast(I32), 0)
         y = [tile("y%d" % t, [P, Y_WINDOW], F32) for t in range(PACK)]
-        for t in range(PACK):
+        for t in range(PACK - 1):
             nc.vector.memset(y[t][:, S:Y_WINDOW], 0.0)
         s = tile("s", [P, (PACK + 1) * S], F32)
         nc.vector.memset(s[:, PACK * S :], 0.0)
@@ -63,20 +61,25 @@ def tile_picked_hcandgclipmix_none_po_kernel(
         nc.sync.dma_start(x_bytes[0:P:8, :].bitcast(I32), x_scales[0].bitcast(I32))
         w_codes = tile("w_codes", [P, 2 * H], U8)
         nc.sync.dma_start(w_codes[:].bitcast(I32), w1_words[0].bitcast(I32))
+        cand_t = load_list("cand_t", cand)
         x_codes = tile("x_codes", [P, T], I32)
         nc.sync.dma_start(x_codes[:], x_words[0].rearrange("p n r -> p (n r)").bitcast(I32))
-        cand_t = load_list("cand_t", cand)
         n1_t = load_list("n1_t", n1)
         for q in range(4):
-            nc.scalar.dma_start(
+            queue = nc.gpsimd if q == 0 else nc.scalar
+            queue.dma_start(
                 w_bytes[32 * q : 32 * q + 4, :].bitcast(I32), w1_scales[0, 4 * q : 4 * q + 4, :].bitcast(I32)
             )
         gs_t = tile("gs_t", [P, PACK], F32)
         nc.gpsimd.dma_start(gs_t[:], gs.rearrange("(p t) o -> p (t o)", t=PACK))
 
+        nc.scalar.activation(y[PACK - 1][:, S:Y_WINDOW], y[0][:, S:Y_WINDOW], COPY)
+
         xq_bytes = tile("xq_bytes", [P, S], U8)
         nc.vector.tensor_copy(xq_bytes[:], x_bytes[:].indirect(offs_t[:]))
-        place_scale_rows((nc.scalar, nc.sync), xq_plane, xq_bytes)
+        xq_plane = tile("xq_plane", [P, S], U8)
+        nc.vector.tensor_copy(xq_plane[:].bitcast(I32), xq_bytes[:].bitcast(I32))
+        close_up_rows(xq_plane, xq_bytes)
 
         w_dealt = tile("w_dealt", [P, 2 * H], U8)
         nc.vector.tensor_copy(
@@ -93,12 +96,12 @@ def tile_picked_hcandgclipmix_none_po_kernel(
 
         xc_bytes = tile("xc_bytes", [P, C], U8)
         nc.vector.tensor_copy(xc_bytes[:], x_bytes[:].indirect(cand_t[:]))
-        xc_bytes_dealt = tile("xc_bytes_dealt", [P, C], U8)
+        xc_plane = tile("xc_plane", [P, C], U8)
         nc.vector.tensor_copy(
-            xc_bytes_dealt[:].rearrange("p (t m) -> p m t", t=PACK),
+            xc_plane[:].rearrange("p (t m) -> p m t", t=PACK),
             xc_bytes[:].rearrange("p (m t) -> p m t", t=PACK),
         )
-        place_scale_rows((nc.sync,), xc_plane, xc_bytes_dealt)
+        close_up_rows(xc_plane, xc_plane)
 
         y_banks = []
         for t in range(PACK):
@@ -113,6 +116,8 @@ def tile_picked_hcandgclipmix_none_po_kernel(
                 stop=True,
             )
             y_banks.append(y_bank)
+            if t in Y_TILES_ON_VECTOR:
+                nc.vector.tensor_scalar(y[t][:, 0:S], y_bank[:], gs_t[:, t : t + 1], None, ALU.mult)
 
         xc_codes = tile("xc_codes", [P, C], U32)
         nc.vector.tensor_copy(xc_codes[:], x_codes[:].bitcast(U32).indirect(cand_t[:]))
@@ -174,7 +179,7 @@ def tile_picked_hcandgclipmix_none_po_kernel(
         steps = [(t, 0, HALF) for t in range(PACK)] + [(t, HALF, HALF) for t in range(PACK - 1)]
         steps = steps + [(PACK - 1, HALF, QUARTER), (PACK - 1, HALF + QUARTER, QUARTER)]
         for i, (t, j0, n) in enumerate(steps):
-            if j0 == 0:
+            if j0 == 0 and t not in Y_TILES_ON_VECTOR:
                 nc.scalar.activation(y[t][:, 0:S], y_banks[t][:], COPY, scale=gs_t[:, t : t + 1])
             pairs = pair_up(t, j0, n)
             if i > 0:
@@ -191,14 +196,13 @@ def tile_picked_hcandgclipmix_none_po_kernel(
         quantise(HALF + QUARTER, QUARTER)
 
         s_rows = s[:, 0 : PACK * S].rearrange("p (t j) -> p t j", t=PACK)
-        for h in range(2):
-            cols = slice(h * HALF, (h + 1) * HALF)
-            for pair in range(2):
-                s_bank = psum.tile([P, 2, HALF], F32, name="s_bank%d%d" % (h, pair))
-                for u in range(2):
-                    t = 2 * pair + u
+        for half in range(2):
+            cols = slice(half * HALF, (half + 1) * HALF)
+            for t0 in (0, 2):
+                s_bank = psum.tile([P, 2, HALF], F32, name="s_bank%d%d" % (half, t0 // 2))
+                for t in (t0, t0 + 1):
                     nc.tensor.matmul_mx(
-                        out=s_bank[:, u, :],
+                        out=s_bank[:, t - t0, :],
                         lhsT=xc_dealt[:, P * t : P * (t + 1)].bitcast(FP8X4),
                         lhsT_scale=xc_plane[:, P * t : P * (t + 1)],
                         rhs=z_codes[:, cols].bitcast(FP8X4),
@@ -206,10 +210,10 @@ def tile_picked_hcandgclipmix_none_po_kernel(
                         start=True,
                         stop=True,
                     )
-                if h == 1 and pair == 1:
-                    nc.vector.tensor_scalar(s_rows[:, 2:4, cols], s_bank[:], 0.0625, None, ALU.mult)
+                if half == 1 and t0 == 2:
+                    nc.vector.tensor_scalar(s_rows[:, t0 : t0 + 2, cols], s_bank[:], 0.0625, None, ALU.mult)
                 else:
-                    nc.scalar.activation(s_rows[:, 2 * pair : 2 * pair + 2, cols], s_bank[:], COPY, scale=0.0625)
+                    nc.scalar.activation(s_rows[:, t0 : t0 + 2, cols], s_bank[:], COPY, scale=0.0625)
 
         out_rows = out_0.rearrange("(p t) j -> p t j", t=PACK)
         out_words = out_1[0].rearrange("p j r -> p (j r)").bitcast(I32)
@@ -221,35 +225,33 @@ def tile_picked_hcandgclipmix_none_po_kernel(
             window = s[:, t * S : (t + 2) * S]
             nc.vector.tensor_copy(s2[:, t, :], window.indirect(n2_t[:]))
             nc.scalar.activation(s3[:, t, :], window.indirect(n3_t[:]), COPY)
-        first = tile("first", [P, PACK, S], F32)
-        nc.vector.tensor_tensor(first[:], s_rows, s2[:], ALU.max)
+        larger_own = tile("first", [P, PACK, S], F32)
+        nc.vector.tensor_tensor(larger_own[:], s_rows, s2[:], ALU.max)
         results = []
-        for h, (j0, n) in enumerate(OUT_PIECES):
+        for piece, (j0, n) in enumerate(OUT_PIECES):
             cols = slice(j0, j0 + n)
             list_cols = slice(j0 // 16, (j0 + n) // 16)
-            s4 = tile("s4_%d" % h, [P, PACK, n], F32)
+            s4 = tile("s4_%d" % piece, [P, PACK, n], F32)
             for t in range(PACK):
                 nc.scalar.activation(s4[:, t, :], s_rows[:, t, :].indirect(n4_t[:, list_cols]), COPY)
-            second = tile("second%d" % h, [P, PACK, n], F32)
-            nc.vector.tensor_tensor(second[:], s3[:, :, cols], s4[:], ALU.max)
-            result = tile("result%d" % h, [P, PACK, n], F32)
-            nc.vector.tensor_tensor(result[:], first[:, :, cols], second[:], ALU.subtract)
+            larger_other = tile("second%d" % piece, [P, PACK, n], F32)
+            nc.vector.tensor_tensor(larger_other[:], s3[:, :, cols], s4[:], ALU.max)
+            result = tile("result%d" % piece, [P, PACK, n], F32)
+            nc.vector.tensor_tensor(result[:], larger_own[:, :, cols], larger_other[:], ALU.subtract)
             nc.sync.dma_start(out_rows[:, :, cols], result[:])
             results.append(result)
-        for h, (j0, n) in enumerate(OUT_PIECES):
-            cols = slice(j0, j0 + n)
-            rounded = tile("rounded%d" % h, [P, n, PACK], BF16)
-            woven = rounded[:].rearrange("p (c i) t -> p c t i", i=4)
-            planar = results[h][:].rearrange("p t (c i) -> p c t i", i=4)
-            if h < len(OUT_PIECES) - 1:
+
+        rounded = tile("rounded", [P, S, PACK], BF16)
+        for piece, (j0, n) in enumerate(OUT_PIECES):
+            woven = rounded[:, j0 : j0 + n, :].rearrange("p (c i) t -> p c t i", i=4)
+            planar = results[piece][:].rearrange("p t (c i) -> p c t i", i=4)
+            if piece < len(OUT_PIECES) - 1:
                 nc.scalar.copy(woven, planar)
             else:
                 nc.vector.tensor_copy(woven, planar)
-            nc.vector.quantize_mx(
-                out=out_codes[:, cols].bitcast(FP8X4),
-                scales=out_plane[:, cols],
-                in_=rounded[:].rearrange("p j t -> p (j t)"),
-            )
+        nc.vector.quantize_mx(
+            out=out_codes[:].bitcast(FP8X4), scales=out_plane[:], in_=rounded[:].rearrange("p j t -> p (j t)")
+        )
         nc.sync.dma_start(out_words, out_codes[:].bitcast(I32))
         for q in range(4):
             queue = nc.sync if q == 3 else nc.scalar

from contextlib import ExitStack

import concourse.mybir as mybir

K, T, S, H, W, C = 512, 2048, 256, 512, 1024, 512
FLOPS = 2 * K * H * S + 2 * K * C * S

F32 = mybir.dt.float32
BF16 = mybir.dt.bfloat16
I32 = mybir.dt.int32
U32 = mybir.dt.uint32
U16 = mybir.dt.uint16
U8 = mybir.dt.uint8
FP8X4 = mybir.dt.float8_e4m3fn_x4
FP4X4 = mybir.dt.float4_e2m1fn_x4
ALU = mybir.AluOpType
COPY = mybir.ActivationFunctionType.Copy

P = 128
PACK = 4
MEMBERS = W // S
HALF = S // 2
QUARTER = S // 4
Y_WINDOW = MEMBERS * HALF + 16
Y_TILES_ON_VECTOR = (1, 2)
OUT_PIECES = ((0, 128), (128, 64), (192, 64))


def tile_picked_hcandgclipmix_none_po_kernel(
    tc, x_words, x_scales, w1_words, w1_scales, gs, offs, n1, cand, n2, n3, n4, out_0, out_1, out_2
):
    nc = tc.nc
    with ExitStack() as ctx:
        keep = ctx.enter_context(tc.tile_pool(name="keep", bufs=1))
        psum = ctx.enter_context(tc.psum_pool(name="psum", bufs=1))

        def tile(name, shape, dtype):
            return keep.tile(shape, dtype, name=name, align_bytes=64)

        def load_list(name, src):
            offsets = keep.tile(list(src.shape), U16, name=name)
            nc.sync.dma_start(offsets[:], src)
            return offsets

        def close_up_rows(plane, spread):
            for i, queue in ((1, nc.sync), (2, nc.scalar), (3, nc.sync)):
                queue.dma_start(plane[i:P:32, :].bitcast(I32), spread[8 * i : P : 32, :].bitcast(I32))

        w_bytes = tile("w_bytes", [P, H], U8)
        nc.gpsimd.memset(w_bytes[:].bitcast(I32), 0)
        x_bytes = tile("x_bytes", [P, T], U8)
        nc.vector.memset(x_bytes[:, : 3 * T // 4].bitcast(I32), 0)
        nc.gpsimd.memset(x_bytes[:, 3 * T // 4 :].bitcast(I32), 0)
        y = [tile("y%d" % t, [P, Y_WINDOW], F32) for t in range(PACK)]
        for t in range(PACK - 1):
            nc.vector.memset(y[t][:, S:Y_WINDOW], 0.0)
        s = tile("s", [P, (PACK + 1) * S], F32)
        nc.vector.memset(s[:, PACK * S :], 0.0)

        offs_t = load_list("offs_t", offs)
        nc.sync.dma_start(x_bytes[0:P:8, :].bitcast(I32), x_scales[0].bitcast(I32))
        w_codes = tile("w_codes", [P, 2 * H], U8)
        nc.sync.dma_start(w_codes[:].bitcast(I32), w1_words[0].bitcast(I32))
        cand_t = load_list("cand_t", cand)
        x_codes = tile("x_codes", [P, T], I32)
        nc.sync.dma_start(x_codes[:], x_words[0].rearrange("p n r -> p (n r)").bitcast(I32))
        n1_t = load_list("n1_t", n1)
        for q in range(4):
            queue = nc.gpsimd if q == 0 else nc.scalar
            queue.dma_start(
                w_bytes[32 * q : 32 * q + 4, :].bitcast(I32), w1_scales[0, 4 * q : 4 * q + 4, :].bitcast(I32)
            )
        gs_t = tile("gs_t", [P, PACK], F32)
        nc.gpsimd.dma_start(gs_t[:], gs.rearrange("(p t) o -> p (t o)", t=PACK))

        nc.scalar.activation(y[PACK - 1][:, S:Y_WINDOW], y[0][:, S:Y_WINDOW], COPY)

        xq_bytes = tile("xq_bytes", [P, S], U8)
        nc.vector.tensor_copy(xq_bytes[:], x_bytes[:].indirect(offs_t[:]))
        xq_plane = tile("xq_plane", [P, S], U8)
        nc.vector.tensor_copy(xq_plane[:].bitcast(I32), xq_bytes[:].bitcast(I32))
        close_up_rows(xq_plane, xq_bytes)

        w_dealt = tile("w_dealt", [P, 2 * H], U8)
        nc.vector.tensor_copy(
            w_dealt[:].rearrange("p (t m b) -> p m t b", t=PACK, b=2),
            w_codes[:].rearrange("p (m t b) -> p m t b", t=PACK, b=2),
        )
        w_plane = tile("w_plane", [P, H], U8)
        nc.gpsimd.tensor_copy(
            w_plane[:].rearrange("p (t m) -> p t m", t=PACK), w_bytes[:].rearrange("p (m t) -> p t m", t=PACK)
        )

        xq_codes = tile("xq_codes", [P, S], U32)
        nc.vector.tensor_copy(xq_codes[:], x_codes[:].bitcast(U32).indirect(offs_t[:]))

        xc_bytes = tile("xc_bytes", [P, C], U8)
        nc.vector.tensor_copy(xc_bytes[:], x_bytes[:].indirect(cand_t[:]))
        xc_plane = tile("xc_plane", [P, C], U8)
        nc.vector.tensor_copy(
            xc_plane[:].rearrange("p (t m) -> p m t", t=PACK),
            xc_bytes[:].rearrange("p (m t) -> p m t", t=PACK),
        )
        close_up_rows(xc_plane, xc_plane)

        y_banks = []
        for t in range(PACK):
            y_bank = psum.tile([P, S], F32, name="y_bank%d" % t)
            nc.tensor.matmul_mx(
                out=y_bank[:],
                lhsT=w_dealt[:, 2 * P * t : 2 * P * (t + 1)].bitcast(FP4X4),
                lhsT_scale=w_plane[:, P * t : P * (t + 1)],
                rhs=xq_codes[:].bitcast(FP8X4),
                rhs_scale=xq_plane[:],
                start=True,
                stop=True,
            )
            y_banks.append(y_bank)
            if t in Y_TILES_ON_VECTOR:
                nc.vector.tensor_scalar(y[t][:, 0:S], y_bank[:], gs_t[:, t : t + 1], None, ALU.mult)

        xc_codes = tile("xc_codes", [P, C], U32)
        nc.vector.tensor_copy(xc_codes[:], x_codes[:].bitcast(U32).indirect(cand_t[:]))
        xc_dealt = tile("xc_dealt", [P, C], U32)
        nc.vector.tensor_copy(
            xc_dealt[:].rearrange("p (t m) -> p m t", t=PACK), xc_codes[:].rearrange("p (m t) -> p m t", t=PACK)
        )

        n2_t = load_list("n2_t", n2)
        n3_t = load_list("n3_t", n3)
        n4_t = load_list("n4_t", n4)

        z_codes = tile("z_codes", [P, S], U32)
        z_plane = tile("z_plane", [P, S], U8)
        capped = tile("capped", [P, PACK, S], F32)
        least = tile("least", [P, PACK, S], F32)
        most = tile("most", [P, PACK, S], F32)
        z = tile("z", [P, S, PACK], BF16)

        def pair_up(t, j0, n):
            name = "%d_%d" % (t, j0)
            members = tile("members" + name, [P, n, 2, 2], F32)
            list_cols = slice(MEMBERS * j0 // 16, MEMBERS * (j0 + n) // 16)
            nc.scalar.activation(
                members[:].rearrange("p j a b -> p (j a b)"), y[t][:].indirect(n1_t[:, list_cols]), COPY
            )
            pair_max = tile("pair_max" + name, [P, n, 2], F32)
            pair_min = tile("pair_min" + name, [P, n, 2], F32)
            nc.vector.tensor_tensor(pair_max[:], members[:, :, 0, :], members[:, :, 1, :], ALU.max)
            nc.vector.tensor_tensor(pair_min[:], members[:, :, 0, :], members[:, :, 1, :], ALU.min)
            return pair_max, pair_min

        def extremes(t, j0, n, pair_max, pair_min):
            cols = slice(j0, j0 + n)
            nc.vector.tensor_tensor(most[:, t, cols], pair_max[:, :, 0], pair_max[:, :, 1], ALU.max)
            nc.vector.tensor_tensor(least[:, t, cols], pair_min[:, :, 0], pair_min[:, :, 1], ALU.min)

        def cap(t, j0, n):
            cols = slice(j0, j0 + n)
            nc.vector.scalar_tensor_tensor(capped[:, t, cols], y[t][:, cols], 1.5, most[:, t, cols], ALU.mult, ALU.min)

        def floor_and_round(j0, n):
            cols = slice(j0, j0 + n)
            nc.vector.tensor_tensor(
                z[:, cols, :].rearrange("p (c i) t -> p c t i", i=4),
                capped[:, :, cols].rearrange("p t (c i) -> p c t i", i=4),
                least[:, :, cols].rearrange("p t (c i) -> p c t i", i=4),
                ALU.max,
            )

        def quantise(j0, n):
            cols = slice(j0, j0 + n)
            nc.vector.quantize_mx(
                out=z_codes[:, cols].bitcast(FP8X4),
                scales=z_plane[:, cols],
                in_=z[:, cols, :].rearrange("p j t -> p (j t)"),
            )

        steps = [(t, 0, HALF) for t in range(PACK)] + [(t, HALF, HALF) for t in range(PACK - 1)]
        steps = steps + [(PACK - 1, HALF, QUARTER), (PACK - 1, HALF + QUARTER, QUARTER)]
        for i, (t, j0, n) in enumerate(steps):
            if j0 == 0 and t not in Y_TILES_ON_VECTOR:
                nc.scalar.activation(y[t][:, 0:S], y_banks[t][:], COPY, scale=gs_t[:, t : t + 1])
            pairs = pair_up(t, j0, n)
            if i > 0:
                cap(*steps[i - 1])
            extremes(t, j0, n, *pairs)
            if i == PACK:
                floor_and_round(0, HALF)
            if i == PACK + 1:
                quantise(0, HALF)
        floor_and_round(HALF, QUARTER)
        cap(*steps[-1])
        quantise(HALF, QUARTER)
        floor_and_round(HALF + QUARTER, QUARTER)
        quantise(HALF + QUARTER, QUARTER)

        s_rows = s[:, 0 : PACK * S].rearrange("p (t j) -> p t j", t=PACK)
        for half in range(2):
            cols = slice(half * HALF, (half + 1) * HALF)
            for t0 in (0, 2):
                s_bank = psum.tile([P, 2, HALF], F32, name="s_bank%d%d" % (half, t0 // 2))
                for t in (t0, t0 + 1):
                    nc.tensor.matmul_mx(
                        out=s_bank[:, t - t0, :],
                        lhsT=xc_dealt[:, P * t : P * (t + 1)].bitcast(FP8X4),
                        lhsT_scale=xc_plane[:, P * t : P * (t + 1)],
                        rhs=z_codes[:, cols].bitcast(FP8X4),
                        rhs_scale=z_plane[:, cols],
                        start=True,
                        stop=True,
                    )
                if half == 1 and t0 == 2:
                    nc.vector.tensor_scalar(s_rows[:, t0 : t0 + 2, cols], s_bank[:], 0.0625, None, ALU.mult)
                else:
                    nc.scalar.activation(s_rows[:, t0 : t0 + 2, cols], s_bank[:], COPY, scale=0.0625)

        out_rows = out_0.rearrange("(p t) j -> p t j", t=PACK)
        out_words = out_1[0].rearrange("p j r -> p (j r)").bitcast(I32)
        out_codes = tile("out_codes", [P, S], U32)
        out_plane = tile("out_plane", [P, S], U8)
        s2 = tile("s2", [P, PACK, S], F32)
        s3 = tile("s3", [P, PACK, S], F32)
        for t in range(PACK):
            window = s[:, t * S : (t + 2) * S]
            nc.vector.tensor_copy(s2[:, t, :], window.indirect(n2_t[:]))
            nc.scalar.activation(s3[:, t, :], window.indirect(n3_t[:]), COPY)
        larger_own = tile("first", [P, PACK, S], F32)
        nc.vector.tensor_tensor(larger_own[:], s_rows, s2[:], ALU.max)
        results = []
        for piece, (j0, n) in enumerate(OUT_PIECES):
            cols = slice(j0, j0 + n)
            list_cols = slice(j0 // 16, (j0 + n) // 16)
            s4 = tile("s4_%d" % piece, [P, PACK, n], F32)
            for t in range(PACK):
                nc.scalar.activation(s4[:, t, :], s_rows[:, t, :].indirect(n4_t[:, list_cols]), COPY)
            larger_other = tile("second%d" % piece, [P, PACK, n], F32)
            nc.vector.tensor_tensor(larger_other[:], s3[:, :, cols], s4[:], ALU.max)
            result = tile("result%d" % piece, [P, PACK, n], F32)
            nc.vector.tensor_tensor(result[:], larger_own[:, :, cols], larger_other[:], ALU.subtract)
            nc.sync.dma_start(out_rows[:, :, cols], result[:])
            results.append(result)

        rounded = tile("rounded", [P, S, PACK], BF16)
        for piece, (j0, n) in enumerate(OUT_PIECES):
            woven = rounded[:, j0 : j0 + n, :].rearrange("p (c i) t -> p c t i", i=4)
            planar = results[piece][:].rearrange("p t (c i) -> p c t i", i=4)
            if piece < len(OUT_PIECES) - 1:
                nc.scalar.copy(woven, planar)
            else:
                nc.vector.tensor_copy(woven, planar)
        nc.vector.quantize_mx(
            out=out_codes[:].bitcast(FP8X4), scales=out_plane[:], in_=rounded[:].rearrange("p j t -> p (j t)")
        )
        nc.sync.dma_start(out_words, out_codes[:].bitcast(I32))
        for q in range(4):
            queue = nc.sync if q == 3 else nc.scalar
            queue.dma_start(
                out_2[0, 4 * q : 4 * q + 4, :].bitcast(I32), out_plane[32 * q : 32 * q + 4, :].bitcast(I32)
            )
